import numpy as np, ml_dtypes
CORES = [125,127,253,255,381,383,509,511]
N = 8
KB, QP = 1, 32
MEM = [2,4]
def setup_inputs(rng):
    return {"q": rng.standard_normal((N, 128, QP), dtype=np.float32).astype(ml_dtypes.bfloat16), "k": rng.standard_normal((N, 128, KB * 128), dtype=np.float32).astype(ml_dtypes.bfloat16), "v": rng.standard_normal((N, 128, KB * 128), dtype=np.float32).astype(ml_dtypes.bfloat16)}
def setup_inputs_big(rng):
    d = setup_inputs(rng)
    for k in ("q", "k", "v"): d[k] = (d[k].astype(np.float32) * 1024.0).astype(d[k].dtype)
    return d
def setup_inputs_small(rng):
    d = setup_inputs(rng)
    for k in ("q", "k", "v"): d[k] = (d[k].astype(np.float32) * (1 / 1024.0)).astype(d[k].dtype)
    return d
def setup_inputs_apart(rng):
    d = setup_inputs(rng)
    f = (10.0 ** rng.permutation(np.linspace(-1.5, 1.5, N))).astype(np.float32).reshape(N, 1, 1)
    for k in ("q", "k", "v"): d[k] = (d[k].astype(np.float32) * f).astype(d[k].dtype)
    return d
def reference(q, k, v):
    Q, K, V = q.astype(np.float64), k.astype(np.float64), v.astype(np.float64)
    y = np.zeros((N, 128, QP))
    for r in range(N):
        for j in MEM:
            for b in range(KB):
                S = np.maximum(K[j][:, 128 * b:128 * b + 128].T @ Q[r], 0.0)
                y[r] += V[j][:, 128 * b:128 * b + 128].T @ S
    return {"y": y.astype(ml_dtypes.bfloat16 if q.dtype != np.float64 else np.float64)}

@@ -1,0 +1,151 @@
+from concourse.bass import DstId, RemoteDMATransfer
+from concourse.mybir import AluOpType
+
+QP = 32
+KP = 128
+GROUP = 4
+Q_ENGINES = 8
+
+SCRATCH = {
+    "kv_own": ("sbuf", [128, 2 * KP], "bfloat16"),
+    "kv_peer": ("sbuf", [128, 2 * KP], "bfloat16"),
+    "q_all": ("sbuf", [128, GROUP * QP], "bfloat16"),
+    "zero": ("sbuf", [128, GROUP * QP], "float32"),
+    "s_own": ("sbuf", [128, GROUP * QP], "bfloat16"),
+    "s_peer": ("sbuf", [128, GROUP * QP], "bfloat16"),
+    "o": ("sbuf", [128, GROUP * QP], "bfloat16"),
+    "q_stage": ("dram", [128, QP], "bfloat16"),
+    "y_land": ("dram", [128, QP], "bfloat16"),
+    "ps_own": ("psum", [128, 512], "float32"),
+    "ps_peer": ("psum", [128, 512], "float32"),
+    "ps_o": ("psum", [128, 512], "float32"),
+}
+SEMAPHORES = ["kv_ld", "q_ld", "q_in", "kv_in", "z_set", "m_own", "m_peer", "r_own", "r_peer", "m_o", "o_cp",
+              "sent", "y_in", "y_st"]
+
+
+def _engines(mask):
+    return [e for e in range(mask.bit_length()) if (mask >> e) & 1]
+
+
+def _bits(engines):
+    m = 0
+    for e in engines:
+        m |= 1 << e
+    return m
+
+
+def _pow2_floor(n):
+    return 1 << (n.bit_length() - 1)
+
+
+def _same_chip(topo, a, b):
+    return topo.host(a) == topo.host(b) and topo.chip(a) == topo.chip(b)
+
+
+def _q_engines(topo, src, hub):
+    return _engines(topo.mask(src, hub))[:Q_ENGINES]
+
+
+def _back_plan(topo, hub, group):
+    far = [c for c in group if c != hub and not _same_chip(topo, hub, c)]
+    near = [c for c in group if c != hub and _same_chip(topo, hub, c)]
+    plan, used = {}, []
+    if far:
+        es = _engines(topo.mask(hub, far[0]))
+        per = _pow2_floor(len(es) // len(far))
+        for i, c in enumerate(far):
+            plan[c] = es[i * per:(i + 1) * per]
+            used += plan[c]
+    if near:
+        es = [e for e in _engines(topo.mask(hub, near[0])) if e not in used]
+        per = _pow2_floor(len(es) // len(near))
+        for i, c in enumerate(near):
+            plan[c] = es[i * per:(i + 1) * per]
+    return far, near, plan
+
+
+def rank_program(g, core, T, topo):
+    if T.rank_of(core) is None:
+        return
+    sem = T.sem
+    cores = list(T.cores)
+    hubs = [cores[j] for j in T.tables["MEM"]]
+
+    def hub_of(c):
+        return [h for h in hubs if topo.rack(topo.host(h)) == topo.rack(topo.host(c))][0]
+
+    hub = hub_of(core)
+    group = [c for c in cores if hub_of(c) == hub]
+    far, near, back = _back_plan(topo, hub, group)
+
+    def cols(c):
+        i = group.index(c)
+        return slice(i * QP, (i + 1) * QP)
+
+    if core != hub:
+        es = _q_engines(topo, core, hub)
+        g.sync.dma_start(T.q_stage[:], T.q[:]).then_inc(sem.q_ld, 16)
+        g.wait_ge(sem.q_ld, 16)
+        rid, pid = topo.addr(hub, core)
+        g.remote_dma(out_ap=T.q_all[:, cols(core)], in_ap=T.q_stage[:], remote_sem=sem.q_in, local_sem=sem.sent,
+                     pid=pid, routing_id=rid, dma_engine_mask=_bits(es))
+        g.sync.wait_ge(sem.y_in, len(back[core]))
+        g.sync.dma_start(T.y[:], T.y_land[:]).then_inc(sem.y_st, 16)
+        g.sync.wait_ge(sem.y_st, 16)
+        g.wait_ge(sem.sent, len(es))
+        return
+
+    peer = [h for h in hubs if h != core][0]
+    k_own, v_own = T.kv_own[:, 0:KP], T.kv_own[:, KP:2 * KP]
+    k_peer, v_peer = T.kv_peer[:, 0:KP], T.kv_peer[:, KP:2 * KP]
+    W = GROUP * QP
+
+    g.sync.dma_start(k_own, T.k[:]).then_inc(sem.kv_ld, 16)
+    g.scalar.dma_start(v_own, T.v[:]).then_inc(sem.kv_ld, 16)
+    g.sync.dma_start(T.q_all[:, cols(core)], T.q[:]).then_inc(sem.q_in, 16)
+    g.vector.memset(T.zero[:], 0.0).then_inc(sem.z_set, 1)
+
+    kv_es = _engines(topo.mask(core, peer))
+    rid, pid = topo.addr(peer, core)
+    g.wait_ge(sem.kv_ld, 32)
+    g.remote_dma(out_ap=T.kv_peer[:], in_ap=T.kv_own[:], remote_sem=sem.kv_in, local_sem=sem.sent,
+                 pid=pid, routing_id=rid, dma_engine_mask=_bits(kv_es))
+    sent = len(kv_es)
+
+    q_total = 16 + sum(len(_q_engines(topo, c, core)) for c in group if c != core)
+    te = g.tensor
+    te.wait_ge(sem.kv_ld, 32)
+    te.wait_ge(sem.q_in, q_total)
+    te.matmul(T.ps_own[:, 0:W], k_own, T.q_all[:], True, True).then_inc(sem.m_own, 1)
+    te.wait_ge(sem.kv_in, len(_engines(topo.mask(peer, core))))
+    te.matmul(T.ps_peer[:, 0:W], k_peer, T.q_all[:], True, True).then_inc(sem.m_peer, 1)
+    te.wait_ge(sem.r_own, 1)
+    te.matmul(T.ps_o[:, 0:W], v_own, T.s_own[:], True, False)
+    te.wait_ge(sem.r_peer, 1)
+    te.matmul(T.ps_o[:, 0:W], v_peer, T.s_peer[:], False, True).then_inc(sem.m_o, 1)
+
+    ve = g.vector
+    ve.wait_ge(sem.z_set, 1)
+    ve.wait_ge(sem.m_own, 1)
+    ve.tensor_tensor(T.s_own[:], T.ps_own[:, 0:W], T.zero[:], AluOpType.max).then_inc(sem.r_own, 1)
+    ve.wait_ge(sem.m_peer, 1)
+    ve.tensor_tensor(T.s_peer[:], T.ps_peer[:, 0:W], T.zero[:], AluOpType.max).then_inc(sem.r_peer, 1)
+    ve.wait_ge(sem.m_o, 1)
+    ve.tensor_copy(T.o[:], T.ps_o[:, 0:W]).then_inc(sem.o_cp, 1)
+
+    g.wait_ge(sem.o_cp, 1)
+    for batch in (far, near):
+        if not batch:
+            continue
+        transfers = []
+        for c in batch:
+            rid, pid = topo.addr(c, core)
+            transfers.append(RemoteDMATransfer(dst_ids=[DstId(rid=rid, pnc=pid)], dma_engine_mask=_bits(back[c]),
+                                               remote_sem=sem.y_in, src=T.o[:, cols(c)], dst=T.y_land[:]))
+            sent += len(back[c])
+        g.remote_dma_fused(transfers, local_sem=sem.sent)
+    g.sync.wait_ge(sem.o_cp, 1)
+    g.sync.dma_start(T.y[:], T.o[:, cols(core)]).then_inc(sem.y_st, 16)
+    g.sync.wait_ge(sem.y_st, 16)
+    g.wait_ge(sem.sent, sent)

@@ -17,11 +17,13 @@ SCRATCH = {
     "q_stage": ("dram", [128, QP], "bfloat16"),
     "y_land": ("dram", [128, QP], "bfloat16"),
     "ps_own": ("psum", [128, 512], "float32"),
-    "ps_peer": ("psum", [128, 512], "float32"),
-    "ps_o": ("psum", [128, 512], "float32"),
+    "ps_pa": ("psum", [128, 512], "float32"),
+    "ps_pb": ("psum", [128, 512], "float32"),
+    "ps_oa": ("psum", [128, 512], "float32"),
+    "ps_ob": ("psum", [128, 512], "float32"),
 }
-SEMAPHORES = ["kv_ld", "q_ld", "q_in", "kv_in", "z_set", "m_own", "m_peer", "r_own", "r_peer", "m_o", "o_cp",
-              "sent", "y_in", "y_st"]
+SEMAPHORES = ["k_ld", "v_ld", "q_ld", "q_in", "k_in", "v_in", "z_set", "m_own", "r_own", "m_pa", "m_pb", "r_pa", "r_pb",
+              "m_oa", "m_ob", "cp_a", "cp_b", "sent", "y_in", "y_st"]
 
 
 def _engines(mask):
@@ -76,8 +78,8 @@ def rank_program(g, core, T, topo):
         return [h for h in hubs if topo.rack(topo.host(h)) == topo.rack(topo.host(c))][0]
 
     hub = hub_of(core)
-    group = [c for c in cores if hub_of(c) == hub]
-    far, near, back = _back_plan(topo, hub, group)
+    far, near, back = _back_plan(topo, hub, [c for c in cores if hub_of(c) == hub])
+    group = far + near + [hub]
 
     def cols(c):
         i = group.index(c)
@@ -100,44 +102,57 @@ def rank_program(g, core, T, topo):
     k_own, v_own = T.kv_own[:, 0:KP], T.kv_own[:, KP:2 * KP]
     k_peer, v_peer = T.kv_peer[:, 0:KP], T.kv_peer[:, KP:2 * KP]
     W = GROUP * QP
+    A = len(far) * QP
 
-    g.sync.dma_start(k_own, T.k[:]).then_inc(sem.kv_ld, 16)
-    g.scalar.dma_start(v_own, T.v[:]).then_inc(sem.kv_ld, 16)
+    g.sync.dma_start(k_own, T.k[:]).then_inc(sem.k_ld, 16)
+    g.scalar.dma_start(v_own, T.v[:]).then_inc(sem.v_ld, 16)
     g.sync.dma_start(T.q_all[:, cols(core)], T.q[:]).then_inc(sem.q_in, 16)
     g.vector.memset(T.zero[:], 0.0).then_inc(sem.z_set, 1)
 
     kv_es = _engines(topo.mask(core, peer))
+    n_in = len(_engines(topo.mask(peer, core)))
     rid, pid = topo.addr(peer, core)
-    g.wait_ge(sem.kv_ld, 32)
-    g.remote_dma(out_ap=T.kv_peer[:], in_ap=T.kv_own[:], remote_sem=sem.kv_in, local_sem=sem.sent,
+    g.wait_ge(sem.k_ld, 16)
+    g.remote_dma(out_ap=k_peer, in_ap=k_own, remote_sem=sem.k_in, local_sem=sem.sent,
                  pid=pid, routing_id=rid, dma_engine_mask=_bits(kv_es))
-    sent = len(kv_es)
+    g.wait_ge(sem.v_ld, 16)
+    g.remote_dma(out_ap=v_peer, in_ap=v_own, remote_sem=sem.v_in, local_sem=sem.sent,
+                 pid=pid, routing_id=rid, dma_engine_mask=_bits(kv_es))
+    sent = 2 * len(kv_es)
 
     q_total = 16 + sum(len(_q_engines(topo, c, core)) for c in group if c != core)
     te = g.tensor
-    te.wait_ge(sem.kv_ld, 32)
+    te.wait_ge(sem.k_ld, 16)
     te.wait_ge(sem.q_in, q_total)
     te.matmul(T.ps_own[:, 0:W], k_own, T.q_all[:], True, True).then_inc(sem.m_own, 1)
-    te.wait_ge(sem.kv_in, len(_engines(topo.mask(peer, core))))
-    te.matmul(T.ps_peer[:, 0:W], k_peer, T.q_all[:], True, True).then_inc(sem.m_peer, 1)
+    te.wait_ge(sem.v_ld, 16)
     te.wait_ge(sem.r_own, 1)
-    te.matmul(T.ps_o[:, 0:W], v_own, T.s_own[:], True, False)
-    te.wait_ge(sem.r_peer, 1)
-    te.matmul(T.ps_o[:, 0:W], v_peer, T.s_peer[:], False, True).then_inc(sem.m_o, 1)
+    te.matmul(T.ps_oa[:, 0:A], v_own, T.s_own[:, 0:A], True, False)
+    te.matmul(T.ps_ob[:, 0:W - A], v_own, T.s_own[:, A:W], True, False)
+    te.wait_ge(sem.k_in, n_in)
+    te.matmul(T.ps_pa[:, 0:A], k_peer, T.q_all[:, 0:A], True, True).then_inc(sem.m_pa, 1)
+    te.matmul(T.ps_pb[:, 0:W - A], k_peer, T.q_all[:, A:W], True, True).then_inc(sem.m_pb, 1)
+    te.wait_ge(sem.v_in, n_in)
+    te.wait_ge(sem.r_pa, 1)
+    te.matmul(T.ps_oa[:, 0:A], v_peer, T.s_peer[:, 0:A], False, True).then_inc(sem.m_oa, 1)
+    te.wait_ge(sem.r_pb, 1)
+    te.matmul(T.ps_ob[:, 0:W - A], v_peer, T.s_peer[:, A:W], False, True).then_inc(sem.m_ob, 1)
 
     ve = g.vector
     ve.wait_ge(sem.z_set, 1)
     ve.wait_ge(sem.m_own, 1)
     ve.tensor_tensor(T.s_own[:], T.ps_own[:, 0:W], T.zero[:], AluOpType.max).then_inc(sem.r_own, 1)
-    ve.wait_ge(sem.m_peer, 1)
-    ve.tensor_tensor(T.s_peer[:], T.ps_peer[:, 0:W], T.zero[:], AluOpType.max).then_inc(sem.r_peer, 1)
-    ve.wait_ge(sem.m_o, 1)
-    ve.tensor_copy(T.o[:], T.ps_o[:, 0:W]).then_inc(sem.o_cp, 1)
+    ve.wait_ge(sem.m_pa, 1)
+    ve.tensor_tensor(T.s_peer[:, 0:A], T.ps_pa[:, 0:A], T.zero[:, 0:A], AluOpType.max).then_inc(sem.r_pa, 1)
+    ve.wait_ge(sem.m_pb, 1)
+    ve.tensor_tensor(T.s_peer[:, A:W], T.ps_pb[:, 0:W - A], T.zero[:, A:W], AluOpType.max).then_inc(sem.r_pb, 1)
+    ve.wait_ge(sem.m_oa, 1)
+    ve.tensor_copy(T.o[:, 0:A], T.ps_oa[:, 0:A]).then_inc(sem.cp_a, 1)
+    ve.wait_ge(sem.m_ob, 1)
+    ve.tensor_copy(T.o[:, A:W], T.ps_ob[:, 0:W - A]).then_inc(sem.cp_b, 1)
 
-    g.wait_ge(sem.o_cp, 1)
-    for batch in (far, near):
-        if not batch:
-            continue
+    for batch, ready in ((far, sem.cp_a), (near, sem.cp_b)):
+        g.wait_ge(ready, 1)
         transfers = []
         for c in batch:
             rid, pid = topo.addr(c, core)
@@ -145,7 +160,7 @@ def rank_program(g, core, T, topo):
                                                remote_sem=sem.y_in, src=T.o[:, cols(c)], dst=T.y_land[:]))
             sent += len(back[c])
         g.remote_dma_fused(transfers, local_sem=sem.sent)
-    g.sync.wait_ge(sem.o_cp, 1)
+    g.sync.wait_ge(sem.cp_b, 1)
     g.sync.dma_start(T.y[:], T.o[:, cols(core)]).then_inc(sem.y_st, 16)
     g.sync.wait_ge(sem.y_st, 16)
     g.wait_ge(sem.sent, sent)

@@ -3,27 +3,25 @@ from concourse.mybir import AluOpType
 
 QP = 32
 KP = 128
-GROUP = 4
-Q_ENGINES = 8
+W = 4 * QP
 
 SCRATCH = {
-    "kv_own": ("sbuf", [128, 2 * KP], "bfloat16"),
-    "kv_peer": ("sbuf", [128, 2 * KP], "bfloat16"),
-    "q_all": ("sbuf", [128, GROUP * QP], "bfloat16"),
-    "zero": ("sbuf", [128, GROUP * QP], "float32"),
-    "s_own": ("sbuf", [128, GROUP * QP], "bfloat16"),
-    "s_peer": ("sbuf", [128, GROUP * QP], "bfloat16"),
-    "o": ("sbuf", [128, GROUP * QP], "bfloat16"),
+    "kv": ("sbuf", [128, 2 * KP], "bfloat16"),
+    "q_all": ("sbuf", [128, W], "bfloat16"),
+    "zero": ("sbuf", [128, W], "float32"),
+    "s": ("sbuf", [128, W], "bfloat16"),
+    "o": ("sbuf", [128, W], "bfloat16"),
+    "a_land": ("sbuf", [128, QP], "bfloat16"),
+    "b_land": ("sbuf", [128, QP], "bfloat16"),
+    "y_sb": ("sbuf", [128, QP], "bfloat16"),
     "q_stage": ("dram", [128, QP], "bfloat16"),
-    "y_land": ("dram", [128, QP], "bfloat16"),
-    "ps_own": ("psum", [128, 512], "float32"),
-    "ps_pa": ("psum", [128, 512], "float32"),
-    "ps_pb": ("psum", [128, 512], "float32"),
+    "ps_sa": ("psum", [128, 512], "float32"),
+    "ps_sb": ("psum", [128, 512], "float32"),
     "ps_oa": ("psum", [128, 512], "float32"),
     "ps_ob": ("psum", [128, 512], "float32"),
 }
-SEMAPHORES = ["k_ld", "v_ld", "q_ld", "q_in", "k_in", "v_in", "z_set", "m_own", "r_own", "m_pa", "m_pb", "r_pa", "r_pb",
-              "m_oa", "m_ob", "cp_a", "cp_b", "sent", "y_in", "y_st"]
+SEMAPHORES = ["k_ld", "v_ld", "q_ld", "q_in", "k_in", "v_in", "z_set", "m_sa", "m_sb", "r_sa", "r_sb",
+              "m_oa", "m_ob", "cp_a", "cp_n", "sent", "a_in", "b_in", "y_rdy", "y_st"]
 
 
 def _engines(mask):
@@ -37,130 +35,154 @@ def _bits(engines):
     return m
 
 
-def _pow2_floor(n):
-    return 1 << (n.bit_length() - 1)
+def _layout(T, topo):
+    cores = list(T.cores)
+    mem = [cores[j] for j in T.tables["MEM"]]
+    hosts = sorted(set(topo.host(c) for c in cores))
+    ranks = {h: [c for c in cores if topo.host(c) == h] for h in hosts}
+    server = {h: ([c for c in ranks[h] if c in mem] + ranks[h])[0] for h in hosts}
+    cabled = {h: [x for x in hosts if topo.rack(x) != topo.rack(h) and topo.may_write(server[h], server[x])][0]
+              for h in hosts}
+    return mem, hosts, ranks, server, cabled
 
 
-def _same_chip(topo, a, b):
-    return topo.host(a) == topo.host(b) and topo.chip(a) == topo.chip(b)
+def _q_plan(topo, c, own, far):
+    off = _engines(topo.mask(c, far))
+    if c == own:
+        return {far: off}
+    half = off[:len(off) // 2]
+    return {far: half, own: [e for e in _engines(topo.mask(c, own)) if e not in half][:len(half)]}
 
 
-def _q_engines(topo, src, hub):
-    return _engines(topo.mask(src, hub))[:Q_ENGINES]
-
-
-def _back_plan(topo, hub, group):
-    far = [c for c in group if c != hub and not _same_chip(topo, hub, c)]
-    near = [c for c in group if c != hub and _same_chip(topo, hub, c)]
-    plan, used = {}, []
-    if far:
-        es = _engines(topo.mask(hub, far[0]))
-        per = _pow2_floor(len(es) // len(far))
-        for i, c in enumerate(far):
-            plan[c] = es[i * per:(i + 1) * per]
-            used += plan[c]
-    if near:
-        es = [e for e in _engines(topo.mask(hub, near[0])) if e not in used]
-        per = _pow2_floor(len(es) // len(near))
-        for i, c in enumerate(near):
-            plan[c] = es[i * per:(i + 1) * per]
-    return far, near, plan
+def _back_plan(topo, srv, far, near):
+    off = _engines(topo.mask(srv, far[0]))
+    per = len(off) // len(far)
+    plan = {c: off[i * per:(i + 1) * per] for i, c in enumerate(far)}
+    for c in near:
+        plan[c] = [e for e in _engines(topo.mask(srv, c)) if e not in off][:len(off)]
+    return plan
 
 
 def rank_program(g, core, T, topo):
     if T.rank_of(core) is None:
         return
     sem = T.sem
-    cores = list(T.cores)
-    hubs = [cores[j] for j in T.tables["MEM"]]
+    mem, hosts, ranks, server, cabled = _layout(T, topo)
+    h = topo.host(core)
+    own, far_srv = server[h], server[cabled[h]]
+    sent = 0
 
-    def hub_of(c):
-        return [h for h in hubs if topo.rack(topo.host(h)) == topo.rack(topo.host(c))][0]
+    def clients(srv):
+        hs = topo.host(srv)
+        return list(ranks[cabled[hs]]), [c for c in ranks[hs] if c != srv]
 
-    hub = hub_of(core)
-    far, near, back = _back_plan(topo, hub, [c for c in cores if hub_of(c) == hub])
-    group = far + near + [hub]
-
-    def cols(c):
-        i = group.index(c)
+    def cols(srv, c):
+        fr, nr = clients(srv)
+        i = (fr + nr + [srv]).index(c)
         return slice(i * QP, (i + 1) * QP)
 
-    if core != hub:
-        es = _q_engines(topo, core, hub)
+    fr, nr = clients(far_srv)
+    n_b = len(_back_plan(topo, far_srv, fr, nr)[core])
+    qp = _q_plan(topo, core, own, far_srv)
+
+    def send_q():
+        transfers = []
+        n = 0
+        for dst, es in qp.items():
+            rid, pid = topo.addr(dst, core)
+            transfers.append(RemoteDMATransfer(dst_ids=[DstId(rid=rid, pnc=pid)], dma_engine_mask=_bits(es),
+                                               remote_sem=sem.q_in, src=T.q_stage[:], dst=T.q_all[:, cols(dst, core)]))
+            n += len(es)
+        g.remote_dma_fused(transfers, local_sem=sem.sent)
+        return n
+
+    if core != own:
+        fo, no = clients(own)
+        n_a = len(_back_plan(topo, own, fo, no)[core])
         g.sync.dma_start(T.q_stage[:], T.q[:]).then_inc(sem.q_ld, 16)
         g.wait_ge(sem.q_ld, 16)
-        rid, pid = topo.addr(hub, core)
-        g.remote_dma(out_ap=T.q_all[:, cols(core)], in_ap=T.q_stage[:], remote_sem=sem.q_in, local_sem=sem.sent,
-                     pid=pid, routing_id=rid, dma_engine_mask=_bits(es))
-        g.sync.wait_ge(sem.y_in, len(back[core]))
-        g.sync.dma_start(T.y[:], T.y_land[:]).then_inc(sem.y_st, 16)
+        sent += send_q()
+        g.vector.wait_ge(sem.a_in, n_a)
+        g.vector.wait_ge(sem.b_in, n_b)
+        g.vector.tensor_tensor(T.y_sb[:], T.a_land[:], T.b_land[:], AluOpType.add).then_inc(sem.y_rdy, 1)
+        g.sync.wait_ge(sem.y_rdy, 1)
+        g.sync.dma_start(T.y[:], T.y_sb[:]).then_inc(sem.y_st, 16)
         g.sync.wait_ge(sem.y_st, 16)
-        g.wait_ge(sem.sent, len(es))
+        g.wait_ge(sem.sent, sent)
         return
 
-    peer = [h for h in hubs if h != core][0]
-    k_own, v_own = T.kv_own[:, 0:KP], T.kv_own[:, KP:2 * KP]
-    k_peer, v_peer = T.kv_peer[:, 0:KP], T.kv_peer[:, KP:2 * KP]
-    W = GROUP * QP
+    far, near = clients(core)
+    back = _back_plan(topo, core, far, near)
+    k, v = T.kv[:, 0:KP], T.kv[:, KP:2 * KP]
     A = len(far) * QP
+    N0, N1 = 0, len(near) * QP
+    holds = core in mem
+    src = [m for m in mem if topo.rack(topo.host(m)) == topo.rack(h)][0]
+    te, ve = g.tensor, g.vector
 
-    g.sync.dma_start(k_own, T.k[:]).then_inc(sem.k_ld, 16)
-    g.scalar.dma_start(v_own, T.v[:]).then_inc(sem.v_ld, 16)
-    g.sync.dma_start(T.q_all[:, cols(core)], T.q[:]).then_inc(sem.q_in, 16)
-    g.vector.memset(T.zero[:], 0.0).then_inc(sem.z_set, 1)
+    if holds:
+        g.sync.dma_start(k, T.k[:]).then_inc(sem.k_ld, 16)
+        g.scalar.dma_start(v, T.v[:]).then_inc(sem.v_ld, 16)
+    g.sync.dma_start(T.q_stage[:], T.q[:]).then_inc(sem.q_ld, 16)
+    g.scalar.dma_start(T.q_all[:, cols(core, core)], T.q[:]).then_inc(sem.q_in, 16)
+    ve.memset(T.zero[:], 0.0).then_inc(sem.z_set, 1)
 
-    kv_es = _engines(topo.mask(core, peer))
-    n_in = len(_engines(topo.mask(peer, core)))
-    rid, pid = topo.addr(peer, core)
-    g.wait_ge(sem.k_ld, 16)
-    g.remote_dma(out_ap=k_peer, in_ap=k_own, remote_sem=sem.k_in, local_sem=sem.sent,
-                 pid=pid, routing_id=rid, dma_engine_mask=_bits(kv_es))
-    g.wait_ge(sem.v_ld, 16)
-    g.remote_dma(out_ap=v_peer, in_ap=v_own, remote_sem=sem.v_in, local_sem=sem.sent,
-                 pid=pid, routing_id=rid, dma_engine_mask=_bits(kv_es))
-    sent = 2 * len(kv_es)
+    if holds:
+        mates = [server[x] for x in hosts if x != h and topo.rack(x) == topo.rack(h)]
+        for part, ready, land in ((k, sem.k_ld, sem.k_in), (None, sem.q_ld, None), (v, sem.v_ld, sem.v_in)):
+            g.wait_ge(ready, 16)
+            if part is None:
+                sent += send_q()
+                continue
+            for d in mates:
+                es = _engines(topo.mask(core, d))
+                rid, pid = topo.addr(d, core)
+                g.remote_dma(out_ap=part, in_ap=part, remote_sem=land, local_sem=sem.sent,
+                             pid=pid, routing_id=rid, dma_engine_mask=_bits(es))
+                sent += len(es)
+        k_rdy, v_rdy, n_kv = sem.k_ld, sem.v_ld, 16
+    else:
+        g.wait_ge(sem.q_ld, 16)
+        sent += send_q()
+        k_rdy, v_rdy, n_kv = sem.k_in, sem.v_in, len(_engines(topo.mask(src, core)))
 
-    q_total = 16 + sum(len(_q_engines(topo, c, core)) for c in group if c != core)
-    te = g.tensor
-    te.wait_ge(sem.k_ld, 16)
+    q_total = 16
+    for c in far + near:
+        hc = topo.host(c)
+        q_total += len(_q_plan(topo, c, server[hc], server[cabled[hc]])[core])
+
+    te.wait_ge(k_rdy, n_kv)
     te.wait_ge(sem.q_in, q_total)
-    te.matmul(T.ps_own[:, 0:W], k_own, T.q_all[:], True, True).then_inc(sem.m_own, 1)
-    te.wait_ge(sem.v_ld, 16)
-    te.wait_ge(sem.r_own, 1)
-    te.matmul(T.ps_oa[:, 0:A], v_own, T.s_own[:, 0:A], True, False)
-    te.matmul(T.ps_ob[:, 0:W - A], v_own, T.s_own[:, A:W], True, False)
-    te.wait_ge(sem.k_in, n_in)
-    te.matmul(T.ps_pa[:, 0:A], k_peer, T.q_all[:, 0:A], True, True).then_inc(sem.m_pa, 1)
-    te.matmul(T.ps_pb[:, 0:W - A], k_peer, T.q_all[:, A:W], True, True).then_inc(sem.m_pb, 1)
-    te.wait_ge(sem.v_in, n_in)
-    te.wait_ge(sem.r_pa, 1)
-    te.matmul(T.ps_oa[:, 0:A], v_peer, T.s_peer[:, 0:A], False, True).then_inc(sem.m_oa, 1)
-    te.wait_ge(sem.r_pb, 1)
-    te.matmul(T.ps_ob[:, 0:W - A], v_peer, T.s_peer[:, A:W], False, True).then_inc(sem.m_ob, 1)
+    te.matmul(T.ps_sa[:, 0:A], k, T.q_all[:, 0:A], True, True).then_inc(sem.m_sa, 1)
+    te.matmul(T.ps_sb[:, 0:W - A], k, T.q_all[:, A:W], True, True).then_inc(sem.m_sb, 1)
+    te.wait_ge(v_rdy, n_kv)
+    te.wait_ge(sem.r_sa, 1)
+    te.matmul(T.ps_oa[:, 0:A], v, T.s[:, 0:A], True, True).then_inc(sem.m_oa, 1)
+    te.wait_ge(sem.r_sb, 1)
+    te.matmul(T.ps_ob[:, 0:W - A], v, T.s[:, A:W], True, True).then_inc(sem.m_ob, 1)
 
-    ve = g.vector
     ve.wait_ge(sem.z_set, 1)
-    ve.wait_ge(sem.m_own, 1)
-    ve.tensor_tensor(T.s_own[:], T.ps_own[:, 0:W], T.zero[:], AluOpType.max).then_inc(sem.r_own, 1)
-    ve.wait_ge(sem.m_pa, 1)
-    ve.tensor_tensor(T.s_peer[:, 0:A], T.ps_pa[:, 0:A], T.zero[:, 0:A], AluOpType.max).then_inc(sem.r_pa, 1)
-    ve.wait_ge(sem.m_pb, 1)
-    ve.tensor_tensor(T.s_peer[:, A:W], T.ps_pb[:, 0:W - A], T.zero[:, A:W], AluOpType.max).then_inc(sem.r_pb, 1)
+    ve.wait_ge(sem.m_sa, 1)
+    ve.tensor_tensor(T.s[:, 0:A], T.ps_sa[:, 0:A], T.zero[:, 0:A], AluOpType.max).then_inc(sem.r_sa, 1)
+    ve.wait_ge(sem.m_sb, 1)
+    ve.tensor_tensor(T.s[:, A:W], T.ps_sb[:, 0:W - A], T.zero[:, A:W], AluOpType.max).then_inc(sem.r_sb, 1)
     ve.wait_ge(sem.m_oa, 1)
     ve.tensor_copy(T.o[:, 0:A], T.ps_oa[:, 0:A]).then_inc(sem.cp_a, 1)
     ve.wait_ge(sem.m_ob, 1)
-    ve.tensor_copy(T.o[:, A:W], T.ps_ob[:, 0:W - A]).then_inc(sem.cp_b, 1)
+    ve.tensor_copy(T.o[:, A + N0:A + N1], T.ps_ob[:, N0:N1]).then_inc(sem.cp_n, 1)
+    ve.wait_ge(sem.b_in, n_b)
+    ve.tensor_tensor(T.y_sb[:], T.ps_ob[:, N1:N1 + QP], T.b_land[:], AluOpType.add).then_inc(sem.y_rdy, 1)
 
-    for batch, ready in ((far, sem.cp_a), (near, sem.cp_b)):
+    for batch, ready, land, dst in ((far, sem.cp_a, sem.b_in, T.b_land), (near, sem.cp_n, sem.a_in, T.a_land)):
         g.wait_ge(ready, 1)
         transfers = []
         for c in batch:
             rid, pid = topo.addr(c, core)
             transfers.append(RemoteDMATransfer(dst_ids=[DstId(rid=rid, pnc=pid)], dma_engine_mask=_bits(back[c]),
-                                               remote_sem=sem.y_in, src=T.o[:, cols(c)], dst=T.y_land[:]))
+                                               remote_sem=land, src=T.o[:, cols(core, c)], dst=dst[:]))
             sent += len(back[c])
         g.remote_dma_fused(transfers, local_sem=sem.sent)
-    g.sync.wait_ge(sem.cp_b, 1)
-    g.sync.dma_start(T.y[:], T.o[:, cols(core)]).then_inc(sem.y_st, 16)
+    g.sync.wait_ge(sem.y_rdy, 1)
+    g.sync.dma_start(T.y[:], T.y_sb[:]).then_inc(sem.y_st, 16)
     g.sync.wait_ge(sem.y_st, 16)
     g.wait_ge(sem.sent, sent)

from concourse.bass import DstId, RemoteDMATransfer
from concourse.mybir import AluOpType

QP = 32
KP = 128
W = 4 * QP

SCRATCH = {
    "kv": ("sbuf", [128, 2 * KP], "bfloat16"),
    "q_all": ("sbuf", [128, W], "bfloat16"),
    "zero": ("sbuf", [128, W], "float32"),
    "s": ("sbuf", [128, W], "bfloat16"),
    "o": ("sbuf", [128, W], "bfloat16"),
    "a_land": ("sbuf", [128, QP], "bfloat16"),
    "b_land": ("sbuf", [128, QP], "bfloat16"),
    "y_sb": ("sbuf", [128, QP], "bfloat16"),
    "q_stage": ("dram", [128, QP], "bfloat16"),
    "ps_sa": ("psum", [128, 512], "float32"),
    "ps_sb": ("psum", [128, 512], "float32"),
    "ps_oa": ("psum", [128, 512], "float32"),
    "ps_ob": ("psum", [128, 512], "float32"),
}
SEMAPHORES = ["k_ld", "v_ld", "q_ld", "q_in", "k_in", "v_in", "z_set", "m_sa", "m_sb", "r_sa", "r_sb",
              "m_oa", "m_ob", "cp_a", "cp_n", "sent", "a_in", "b_in", "y_rdy", "y_st"]


def _engines(mask):
    return [e for e in range(mask.bit_length()) if (mask >> e) & 1]


def _bits(engines):
    m = 0
    for e in engines:
        m |= 1 << e
    return m


def _layout(T, topo):
    cores = list(T.cores)
    mem = [cores[j] for j in T.tables["MEM"]]
    hosts = sorted(set(topo.host(c) for c in cores))
    ranks = {h: [c for c in cores if topo.host(c) == h] for h in hosts}
    server = {h: ([c for c in ranks[h] if c in mem] + ranks[h])[0] for h in hosts}
    cabled = {h: [x for x in hosts if topo.rack(x) != topo.rack(h) and topo.may_write(server[h], server[x])][0]
              for h in hosts}
    return mem, hosts, ranks, server, cabled


def _q_plan(topo, c, own, far):
    off = _engines(topo.mask(c, far))
    if c == own:
        return {far: off}
    half = off[:len(off) // 2]
    return {far: half, own: [e for e in _engines(topo.mask(c, own)) if e not in half][:len(half)]}


def _back_plan(topo, srv, far, near):
    off = _engines(topo.mask(srv, far[0]))
    per = len(off) // len(far)
    plan = {c: off[i * per:(i + 1) * per] for i, c in enumerate(far)}
    for c in near:
        plan[c] = [e for e in _engines(topo.mask(srv, c)) if e not in off][:len(off)]
    return plan


def rank_program(g, core, T, topo):
    if T.rank_of(core) is None:
        return
    sem = T.sem
    mem, hosts, ranks, server, cabled = _layout(T, topo)
    h = topo.host(core)
    own, far_srv = server[h], server[cabled[h]]
    sent = 0

    def clients(srv):
        hs = topo.host(srv)
        return list(ranks[cabled[hs]]), [c for c in ranks[hs] if c != srv]

    def cols(srv, c):
        fr, nr = clients(srv)
        i = (fr + nr + [srv]).index(c)
        return slice(i * QP, (i + 1) * QP)

    fr, nr = clients(far_srv)
    n_b = len(_back_plan(topo, far_srv, fr, nr)[core])
    qp = _q_plan(topo, core, own, far_srv)

    def send_q():
        transfers = []
        n = 0
        for dst, es in qp.items():
            rid, pid = topo.addr(dst, core)
            transfers.append(RemoteDMATransfer(dst_ids=[DstId(rid=rid, pnc=pid)], dma_engine_mask=_bits(es),
                                               remote_sem=sem.q_in, src=T.q_stage[:], dst=T.q_all[:, cols(dst, core)]))
            n += len(es)
        g.remote_dma_fused(transfers, local_sem=sem.sent)
        return n

    if core != own:
        fo, no = clients(own)
        n_a = len(_back_plan(topo, own, fo, no)[core])
        g.sync.dma_start(T.q_stage[:], T.q[:]).then_inc(sem.q_ld, 16)
        g.wait_ge(sem.q_ld, 16)
        sent += send_q()
        g.vector.wait_ge(sem.a_in, n_a)
        g.vector.wait_ge(sem.b_in, n_b)
        g.vector.tensor_tensor(T.y_sb[:], T.a_land[:], T.b_land[:], AluOpType.add).then_inc(sem.y_rdy, 1)
        g.sync.wait_ge(sem.y_rdy, 1)
        g.sync.dma_start(T.y[:], T.y_sb[:]).then_inc(sem.y_st, 16)
        g.sync.wait_ge(sem.y_st, 16)
        g.wait_ge(sem.sent, sent)
        return

    far, near = clients(core)
    back = _back_plan(topo, core, far, near)
    k, v = T.kv[:, 0:KP], T.kv[:, KP:2 * KP]
    A = len(far) * QP
    N0, N1 = 0, len(near) * QP
    holds = core in mem
    src = [m for m in mem if topo.rack(topo.host(m)) == topo.rack(h)][0]
    te, ve = g.tensor, g.vector

    if holds:
        g.sync.dma_start(k, T.k[:]).then_inc(sem.k_ld, 16)
        g.scalar.dma_start(v, T.v[:]).then_inc(sem.v_ld, 16)
    g.sync.dma_start(T.q_stage[:], T.q[:]).then_inc(sem.q_ld, 16)
    g.scalar.dma_start(T.q_all[:, cols(core, core)], T.q[:]).then_inc(sem.q_in, 16)
    ve.memset(T.zero[:], 0.0).then_inc(sem.z_set, 1)

    if holds:
        mates = [server[x] for x in hosts if x != h and topo.rack(x) == topo.rack(h)]
        for part, ready, land in ((k, sem.k_ld, sem.k_in), (None, sem.q_ld, None), (v, sem.v_ld, sem.v_in)):
            g.wait_ge(ready, 16)
            if part is None:
                sent += send_q()
                continue
            for d in mates:
                es = _engines(topo.mask(core, d))
                rid, pid = topo.addr(d, core)
                g.remote_dma(out_ap=part, in_ap=part, remote_sem=land, local_sem=sem.sent,
                             pid=pid, routing_id=rid, dma_engine_mask=_bits(es))
                sent += len(es)
        k_rdy, v_rdy, n_kv = sem.k_ld, sem.v_ld, 16
    else:
        g.wait_ge(sem.q_ld, 16)
        sent += send_q()
        k_rdy, v_rdy, n_kv = sem.k_in, sem.v_in, len(_engines(topo.mask(src, core)))

    q_total = 16
    for c in far + near:
        hc = topo.host(c)
        q_total += len(_q_plan(topo, c, server[hc], server[cabled[hc]])[core])

    te.wait_ge(k_rdy, n_kv)
    te.wait_ge(sem.q_in, q_total)
    te.matmul(T.ps_sa[:, 0:A], k, T.q_all[:, 0:A], True, True).then_inc(sem.m_sa, 1)
    te.matmul(T.ps_sb[:, 0:W - A], k, T.q_all[:, A:W], True, True).then_inc(sem.m_sb, 1)
    te.wait_ge(v_rdy, n_kv)
    te.wait_ge(sem.r_sa, 1)
    te.matmul(T.ps_oa[:, 0:A], v, T.s[:, 0:A], True, True).then_inc(sem.m_oa, 1)
    te.wait_ge(sem.r_sb, 1)
    te.matmul(T.ps_ob[:, 0:W - A], v, T.s[:, A:W], True, True).then_inc(sem.m_ob, 1)

    ve.wait_ge(sem.z_set, 1)
    ve.wait_ge(sem.m_sa, 1)
    ve.tensor_tensor(T.s[:, 0:A], T.ps_sa[:, 0:A], T.zero[:, 0:A], AluOpType.max).then_inc(sem.r_sa, 1)
    ve.wait_ge(sem.m_sb, 1)
    ve.tensor_tensor(T.s[:, A:W], T.ps_sb[:, 0:W - A], T.zero[:, A:W], AluOpType.max).then_inc(sem.r_sb, 1)
    ve.wait_ge(sem.m_oa, 1)
    ve.tensor_copy(T.o[:, 0:A], T.ps_oa[:, 0:A]).then_inc(sem.cp_a, 1)
    ve.wait_ge(sem.m_ob, 1)
    ve.tensor_copy(T.o[:, A + N0:A + N1], T.ps_ob[:, N0:N1]).then_inc(sem.cp_n, 1)
    ve.wait_ge(sem.b_in, n_b)
    ve.tensor_tensor(T.y_sb[:], T.ps_ob[:, N1:N1 + QP], T.b_land[:], AluOpType.add).then_inc(sem.y_rdy, 1)

    for batch, ready, land, dst in ((far, sem.cp_a, sem.b_in, T.b_land), (near, sem.cp_n, sem.a_in, T.a_land)):
        g.wait_ge(ready, 1)
        transfers = []
        for c in batch:
            rid, pid = topo.addr(c, core)
            transfers.append(RemoteDMATransfer(dst_ids=[DstId(rid=rid, pnc=pid)], dma_engine_mask=_bits(back[c]),
                                               remote_sem=land, src=T.o[:, cols(core, c)], dst=dst[:]))
            sent += len(back[c])
        g.remote_dma_fused(transfers, local_sem=sem.sent)
    g.sync.wait_ge(sem.y_rdy, 1)
    g.sync.dma_start(T.y[:], T.y_sb[:]).then_inc(sem.y_st, 16)
    g.sync.wait_ge(sem.y_st, 16)
    g.wait_ge(sem.sent, sent)
